import numpy as np, ml_dtypes
CORES = [2,6,10,14,18,22,26,30]
N = 8
BF = ml_dtypes.bfloat16
def f(rng, *shape):
    return (rng.standard_normal(shape, dtype=np.float32) * np.exp2(rng.integers(-2, 3, shape[:-1] + (1,)))).astype(BF)
def wide(rng, *shape):
    v = f(rng, *shape).astype(np.float32); k = shape[:-2] + (1, shape[-1])
    return (v * np.exp2(rng.integers(-6, 7, k)) * (rng.random(k) > 0.0625)).astype(BF)
P, NT, W, D = 1024, 128, 512, 64
def order(g):
    return range(N)
def places(ln):
    n = np.asarray(ln).reshape(-1, NT).astype(np.int64) + 1; m = len(n)
    t = np.repeat(np.tile(np.arange(NT), m), n.reshape(-1)).reshape(m, P)
    last = np.zeros((m, P), bool); last[np.arange(m)[:, None], np.add.accumulate(n, 1) - 1] = True
    return t, last
def steps(ln, ds):
    t, last = places(ln); m = len(t); src = np.arange(P) - np.take_along_axis(np.asarray(ds).reshape(m, NT).astype(np.int64), t, 1)
    e = np.zeros((m, P), np.int64); row = np.arange(m)
    for i in range(P):
        j = src[:, i]; e[:, i] = np.where(last[:, i], 0, 1 + np.where(j >= 0, e[row, np.maximum(j, 0)], 0))
    return e
def lengths(rng, at, big):
    n = np.zeros((N, 8, NT), np.int64)
    for r in range(N):
        for g in range(8):
            b = int(big[r, g]); rest = P - NT - b
            v = np.minimum(rng.multinomial(rest, rng.dirichlet(np.where(rng.random(NT - 1) < 0.25, 0.001, 1.0))), D)
            v = v + rng.multivariate_hypergeometric(D - v, rest - int(np.sum(v)))
            n[r, g] = np.insert(v, int(at[r, g]), b)
    return n
def starts(n):
    return np.add.accumulate(n + 1, 2) - n - 1
def distances(rng, n):
    s = starts(n); k = rng.integers(0, 4, n.shape)
    over = rng.integers(np.minimum(s, W - 1) + 1, W + 1)
    return np.where(k == 0, rng.integers(1, 9, n.shape), np.where(k == 3, over, rng.integers(1, W + 1, n.shape)))
def inside(rng, n, d, share):
    s = starts(n); d = np.array(d)
    for g in range(8):
        q = order(g)[0]; m = (d[q, g] > s[q, g]) & (s[q, g] > 0) & (rng.random(NT) < share)
        d[q, g] = np.where(m, rng.integers(1, np.maximum(s[q, g], 1) + 1), d[q, g])
    return d
def fit(n, d):
    d = np.array(d)
    for r in range(N):
        for g in range(8):
            e = []
            for t, (c, k) in enumerate(zip(n[r, g].tolist(), d[r, g].tolist())):
                s = len(e)
                for i in range(s, s + c): e.append(1 + (e[i - k] if i >= k else 0))
                if max(e[s:], default=0) > D:
                    d[r, g, t] = 1; e[s:] = range(1, c + 1)
                e.append(0)
    return d
def pack(rng, n, d):
    return {"ln": n.astype(np.int32), "ds": d.astype(np.int32), "le": f(rng, N, 128, NT)}
def setup_inputs(rng):
    n = lengths(rng, rng.integers(0, NT, (N, 8)), rng.integers(1, D + 1, (N, 8)))
    return pack(rng, n, fit(n, inside(rng, n, distances(rng, n), 0.75)))
def setup_inputs_deep(rng):
    at = np.where(rng.random((N, 8)) < 0.25, rng.choice(np.array([0, NT - 1]), (N, 8)), rng.integers(0, NT, (N, 8)))
    n = lengths(rng, at, np.full((N, 8), D)); d = np.where(rng.random(n.shape) < 0.5, rng.integers(1, 4, n.shape), distances(rng, n))
    d = inside(rng, n, d, 0.75); np.put_along_axis(d, at[:, :, None], 1, 2)
    return pack(rng, n, fit(n, d))
def setup_inputs_hops(rng):
    n = lengths(rng, rng.integers(0, NT, (N, 8)), rng.integers(1, D + 1, (N, 8)))
    return pack(rng, n, fit(n, inside(rng, n, rng.integers(W - 8, W + 1, n.shape), 1.0)))
def setup_inputs_ends(rng):
    at = rng.choice(np.array([0, NT - 1]), (N, 8)); at[:, :2] = 0
    n = lengths(rng, at, rng.integers(2, D + 1, (N, 8))); n[rng.integers(0, N)] = P // NT - 1
    s = starts(n); d = np.choose(rng.integers(0, 6, n.shape), [s * 0 + W, s * 0 + 1, s, s + 1, s + n, n])
    d = inside(rng, n, np.minimum(np.maximum(d, 1), W), 0.5); d[:, 0, 0] = W; d[:, 1, 0] = 1
    return pack(rng, n, fit(n, d))
def setup_inputs_long(rng):
    at = rng.integers(0, NT, (N, 8)); k = rng.integers(P // D, W + 1, (N, 8)); u = rng.integers(0, 3, (N, 8)); k = np.where(u == 0, P // D, np.where(u == 1, W, k))
    for g in range(8):
        q = order(g)[0]; at[q, g] = NT - 1; k[q, g] = rng.integers(P // D, min(W, NT - 1) + 1)
    n = np.zeros((N, 8, NT), np.int64); np.put_along_axis(n, at[:, :, None], P - NT, 2)
    d = rng.integers(1, W + 1, n.shape); np.put_along_axis(d, at[:, :, None], k[:, :, None], 2)
    return pack(rng, n, d)
def setup_inputs_spread(rng):
    d = setup_inputs(rng); d["le"] = wide(rng, N, 128, NT); return d
def check_inputs(d):
    bad = []; a = np.asarray(d["ln"]).astype(np.int64); b = np.asarray(d["ds"]).astype(np.int64)
    if (a < 0).any() or (np.sum(a, 2) + NT != P).any(): bad.append("lengths")
    if (b < 1).any() or (b > W).any(): bad.append("distances")
    if not bad and (steps(a, b) > D).any(): bad.append("steps")
    if not np.isfinite(np.asarray(d["le"]).astype(np.float32)).all(): bad.append("finite")
    return bad
def reference(ln, ds, le):
    y = np.zeros((N, 128, P), BF); t, last = places(ln); t = t.reshape(N, 8, P); last = last.reshape(N, 8, P)
    for g in range(8):
        buf = np.zeros((W + P, 16), BF)
        for r in order(g):
            a = np.ascontiguousarray(le[r, 16 * g:16 * g + 16].T); k = ds[r, g][t[r, g]].tolist(); tk = t[r, g].tolist(); own = last[r, g].tolist()
            for i in range(P):
                buf[W + i] = a[tk[i]] if own[i] else buf[W + i - k[i]]
            y[r, 16 * g:16 * g + 16] = buf[W:].T
            buf[:W] = buf[P:]
    return {"y": y}

@@ -1,0 +1,312 @@
+from concourse.bass import DstId, RemoteDMATransfer
+from concourse.mybir import AluOpType, ActivationFunctionType
+
+P, NT, W = 1024, 128, 512
+NL = NT + W
+NC = NL + P
+HALF = 256
+GROUPS = ((0, 2), (2, 4), (4, 7))
+PLAN = (0, 0, 1, 2, 3, 4, 5, 7)
+CUT = 640
+NZ = 10
+
+SCRATCH = {
+    "lnI": ("sbuf", [128, 128], "int32"), "dsI": ("sbuf", [128, 128], "int32"),
+    "lnF": ("sbuf", [128, 128], "float16"), "cum": ("sbuf", [128, 144], "float16"), "X": ("sbuf", [128, 144], "float16"),
+    "pI": ("sbuf", [128, 8], "int32"), "k7I": ("sbuf", [128, 8], "int32"), "rtI": ("sbuf", [128, 8], "int32"),
+    "qgI": ("sbuf", [128, 8], "int32"),
+    "hN": ("sbuf", [128, 8], "float32"), "lN": ("sbuf", [128, 8], "float32"), "s2": ("sbuf", [128, 8], "float32"),
+    "w1": ("sbuf", [128, 8], "float32"), "w": ("sbuf", [128, 8], "float32"), "wN": ("sbuf", [128, 8], "float32"),
+    "lowX": ("sbuf", [128, 8], "float32"), "topX": ("sbuf", [128, 8], "float32"), "bias": ("sbuf", [128, 8], "float32"),
+    "qg": ("sbuf", [128, 8], "float32"), "rt": ("sbuf", [128, 8], "float32"), "pF": ("sbuf", [128, 8], "float32"),
+    "hs": ("sbuf", [128, 16], "float32"),
+    "x1": ("sbuf", [128, 128], "float32"), "c16": ("sbuf", [128, 128], "float32"), "r16": ("sbuf", [128, 128], "float32"),
+    "Sel": ("sbuf", [128, 128], "float16"), "mask": ("sbuf", [128, 128], "bfloat16"), "B": ("sbuf", [128, 8], "float16"),
+    "AA": ("sbuf", [128, 128], "float16"),
+    "wV": ("sbuf", [128, 144], "float32"), "WP": ("sbuf", [128, 144], "float16"), "WM": ("sbuf", [128, 144], "float16"),
+    "qV": ("sbuf", [128, 144], "float32"), "qU": ("sbuf", [128, 144], "float32"), "Q": ("sbuf", [128, 144], "bfloat16"),
+    "tmp": ("sbuf", [128, 144], "bfloat16"), "offs": ("sbuf", [128, 8], "uint16"),
+    "Z": ("sbuf", [128, NC], "bfloat16"),
+    "T0": ("sbuf", [128, NC], "bfloat16"), "T1": ("sbuf", [128, NC], "bfloat16"),
+    "L0": ("sbuf", [128, 64], "uint16"), "L1": ("sbuf", [128, 64], "uint16"), "L2": ("sbuf", [128, 64], "uint16"),
+    "LF": ("sbuf", [128, 64], "uint16"),
+    "M": ("sbuf", [128, 256], "uint16"),
+    "D": ("sbuf", [128, 8 * NL], "bfloat16"),
+    "Y": ("sbuf", [128, P], "bfloat16"),
+    "psA": ("psum", [128, 512], "float32"), "psE": ("psum", [128, 512], "float32"), "psD": ("psum", [128, 512], "float32"),
+    "psW0": ("psum", [128, 512], "float32"), "psW1": ("psum", [128, 512], "float32"), "psW2": ("psum", [128, 512], "float32"),
+    "psW3": ("psum", [128, 512], "float32"),
+}
+SEMAPHORES = ["qv", "qa", "qp", "qg", "ldln", "ldd0", "ldd1", "ldle", "st0", "st1", "lea", "sent"] + ["m%d" % s for s in range(8)]
+
+
+def rank_program(g, core, T, topo):
+    rank = T.rank_of(core)
+    if rank is None:
+        return
+    queue = {"v": g.vector, "a": g.scalar, "p": g.tensor, "g": g, "s": g.sync}
+    known = {e: {} for e in queue}
+    snap = {}
+    count = {}
+    acc = {}
+
+    def await_tokens(e, toks):
+        best = {}
+        for s, v in toks:
+            if known[e].get(s, 0) < v:
+                best[s] = max(best.get(s, 0), v)
+        for s, v in sorted(best.items()):
+            if any(t != s and snap.get((t, best[t]), {}).get(s, 0) >= v for t in best):
+                continue
+            if known[e].get(s, 0) >= v:
+                continue
+            queue[e].wait_ge(T.sem[s], v)
+            known[e][s] = v
+            for t, w in snap.get((s, v), {}).items():
+                known[e][t] = max(known[e].get(t, 0), w)
+
+    def depend(e, reads, writes):
+        toks = []
+        for b, lo, hi in reads:
+            toks += [a[3] for a in acc.get(b, []) if a[2] and a[0] < hi and lo < a[1]]
+        for b, lo, hi in writes:
+            toks += [a[3] for a in acc.get(b, []) if a[0] < hi and lo < a[1]]
+        await_tokens(e, toks)
+
+    def record(e, tok, reads, writes):
+        if e is not None:
+            snap[tok] = dict(known[e])
+            snap[tok][tok[0]] = tok[1]
+        for b, lo, hi in writes:
+            acc[b] = [a for a in acc.get(b, []) if not (lo <= a[0] and a[1] <= hi)] + [[lo, hi, True, tok]]
+        for b, lo, hi in reads:
+            acc.setdefault(b, []).append([lo, hi, False, tok])
+
+    def op(e, call, reads, writes):
+        depend(e, reads, writes)
+        s = "q" + e
+        count[s] = count.get(s, 0) + 1
+        call(queue[e]).then_inc(T.sem[s], 1)
+        record(e, (s, count[s]), reads, writes)
+
+    def dma(e, sem, out, in_, reads, writes):
+        depend(e, reads, writes)
+        count[sem] = count.get(sem, 0) + 16
+        queue[e].dma_start(out, in_).then_inc(T.sem[sem], 16)
+        record(e, (sem, count[sem]), reads, writes)
+
+    later = [c for c in T.cores if T.rank_of(c) > rank]
+    sent = [0]
+
+    def lanes(src, dst):
+        if topo.chip(src) != topo.chip(dst):
+            return topo.engines(src, dst)
+        off = [x for c in T.cores if topo.chip(c) != topo.chip(src) and T.rank_of(c) > T.rank_of(src)
+               for x in topo.engines(src, c)]
+        return [x for x in topo.engines(src, dst) if x not in off]
+
+    def send(cores, name, lo, hi, sem, dst_name, dlo, dhi):
+        if not cores:
+            return
+        depend("g", [(name, lo, hi)], [])
+        sets = []
+        for c in cores:
+            e = lanes(core, c)
+            same = [x for x in sets if x[0] == e]
+            if same:
+                same[0][1].append(c)
+            else:
+                sets.append([e, [c]])
+        trs = []
+        for e, cs in sets:
+            ids = []
+            for c in cs:
+                rid, pid, _ = topo.addr(c)
+                ids.append(DstId(rid=rid, pnc=pid))
+            trs.append(RemoteDMATransfer(dst_ids=ids, dma_engine_mask=sum(1 << x for x in e), remote_sem=T.sem[sem],
+                                         srcs=[T[name][:, lo:hi]], dsts=[T[dst_name][:, dlo:dhi] for _ in cs]))
+            sent[0] += len(e)
+        g.remote_dma_fused(trs, local_sem=T.sem.sent)
+
+    A, F = AluOpType, ActivationFunctionType
+
+    if rank:
+        record(None, ("lea", sum(len(lanes(T.cores[s], core)) for s in range(rank))), [],
+               [("D", NL * s, NL * s + NT) for s in range(rank)])
+        for s in range(rank):
+            record(None, ("m%d" % s, len(lanes(T.cores[s], core))), [], [("M", 32 * s, 32 * s + 32)])
+
+    dma("s", "ldln", T.lnI[0:8, :], T.ln[:], [], [("lnI", 0, 128)])
+    dma("a", "ldd0", T.dsI[0:8, :], T.ds[:], [], [("dsI", 0, 64)])
+    dma("s", "ldd1", T.dsI[8:16, :], T.ds[:], [], [("dsI", 64, 128)])
+    dma("s", "ldle", T.D[:, NL * rank:NL * rank + NT], T.le[:], [], [("D", NL * rank, NL * rank + NT)])
+
+    def iota(name, rows, n, pattern, base, cm):
+        out = T[name][0:rows, 0:n]
+        if name == "pI":
+            op("g", lambda q: q.iota(out, pattern, base, cm), [], [(name, 0, n)])
+        else:
+            op("g", lambda q: q.iota(out, pattern, base, cm, allow_small_or_imprecise_dtypes=True), [], [(name, 0, n)])
+
+    iota("pI", 128, 2, [[0, 2]], 0, 1)
+    iota("c16", 128, 128, [[1, 8], [0, 16]], 0, 0)
+    iota("x1", 128, 128, [[1, 128]], 0, 0)
+    iota("r16", 128, 128, [[0, 8], [1, 16]], 0, 0)
+    iota("wV", 16, 144, [[1, 9], [8, 2], [100, 8]], -100, -1)
+    iota("qV", 128, 144, [[1, 9], [1000, 16]], -1, 0)
+
+    def vs(out, in0, s1, s2, op0, op1, reads, writes):
+        if op1 is None:
+            op("v", lambda q: q.tensor_scalar(out, in0, s1, None, op0), reads, writes)
+        else:
+            op("v", lambda q: q.tensor_scalar(out, in0, s1, s2, op0, op1), reads, writes)
+
+    def act(out, in_, func, reads, writes, bias=0.0, scale=1.0):
+        op("a", lambda q: q.activation(out, in_, func, bias=bias, scale=scale), reads, writes)
+
+    def col(name):
+        return T[name][:, 0:1]
+
+    def one(name):
+        return (name, 0, 1)
+
+    def copy_col(name, src):
+        op("v", lambda q: q.tensor_copy(col(name), col(src)), [one(src)], [one(name)])
+
+    vs(col("k7I"), col("pI"), 7, None, A.bitwise_and, None, [one("pI")], [one("k7I")])
+    vs(col("rtI"), col("pI"), 15, None, A.bitwise_and, None, [one("pI")], [one("rtI")])
+    vs(col("qgI"), col("pI"), 4, None, A.arith_shift_right, None, [one("pI")], [one("qgI")])
+    vs(T.lowX[0:16, 0:2], T.pI[0:16, 0:2], 8.0, float(HALF), A.is_lt, A.mult, [("pI", 0, 2)], [("lowX", 0, 2)])
+    copy_col("pF", "pI")
+    act(T.topX[0:16, 0:1], T.lowX[0:16, 0:1], F.Copy, [one("lowX")], [one("topX")], bias=float(HALF))
+    vs(col("hN"), col("k7I"), 2.0, -1.0, A.is_equal, A.mult, [one("k7I")], [one("hN")])
+    vs(col("lN"), col("k7I"), 3.0, -1.0, A.is_equal, A.mult, [one("k7I")], [one("lN")])
+    vs(col("s2"), col("k7I"), 2.0, None, A.is_lt, None, [one("k7I")], [one("s2")])
+    op("v", lambda q: q.tensor_copy(T.X[0:16, 0:130:129], T.lowX[0:16, 0:2]), [("lowX", 0, 2)], [("X", 0, 1), ("X", 129, 130)])
+    copy_col("rt", "rtI")
+    copy_col("qg", "qgI")
+    vs(T.Sel[0:8, :], T.c16[0:8, :], T.pF[0:8, 0:1], None, A.is_equal, None, [("c16", 0, 128), one("pF")], [("Sel", 0, 128)])
+    vs(T.B[:], T.c16[:, 0:128:16], col("qg"), None, A.is_equal, None, [("c16", 0, 128), one("qg")], [("B", 0, 8)])
+    vs(col("bias"), col("rtI"), 1.0, float(HALF), A.is_equal, A.mult, [one("rtI")], [one("bias")])
+    vs(T.mask[:], T.r16[:], col("rt"), None, A.is_ge, None, [("r16", 0, 128), one("rt")], [("mask", 0, 128)])
+
+    vs(T.lnF[0:8, :], T.lnI[0:8, :], 1.0, None, A.add, None, [("lnI", 0, 128)], [("lnF", 0, 128)])
+    op("p", lambda q: q.matmul(T.psA[:, 0:128], T.lnF[0:8, :], T.Sel[0:8, :], True, True),
+       [("lnF", 0, 128), ("Sel", 0, 128)], [("psA", 0, 512)])
+    vs(T.X[0:16, 1:129], T.dsI[0:16, :], T.lowX[0:16, 0:1], T.topX[0:16, 0:1], A.max, A.min,
+       [("dsI", 0, 128), one("lowX"), one("topX")], [("X", 1, 129)])
+    for name, c in (("WP", 1.0), ("WM", -1.0)):
+        vs(T[name][0:16, :], T.wV[0:16, :], 0.0, c, A.is_equal, A.mult, [("wV", 0, 144)], [(name, 0, 144)])
+    op("v", lambda q: q.tensor_tensor_scan(T.cum[0:8, 16:144], T.lnF[0:8, :], T.lnF[0:8, :], 0.0, A.add, A.max),
+       [("lnF", 0, 128)], [("cum", 16, 144)])
+    op("v", lambda q: q.tensor_tensor(T.AA[:], T.psA[:, 0:128], T.mask[:], A.mult),
+       [("psA", 0, 512), ("mask", 0, 128)], [("AA", 0, 128)])
+
+    act(col("w1"), col("hN"), F.Identity, [one("hN"), one("s2")], [one("w1")], bias=col("s2"), scale=-64.0)
+    act(T.hs[:, 0:13], T.x1[:, 0:13], F.Copy, [("x1", 0, 13), one("hN")], [("hs", 0, 13)], scale=col("hN"))
+    act(T.Z[:, 0:128], T.x1[:], F.Copy, [("x1", 0, 128), one("lN")], [("Z", 0, 128)], scale=col("lN"))
+    act(col("w"), col("lN"), F.Identity, [one("lN"), one("w1")], [one("w")], bias=col("w1"), scale=-0.5)
+
+    def block(e, n):
+        out, r, w = T.Z[:, 128 * n:128 * n + 128], [("Z", 0, 128), ("hs", n, n + 1)], [("Z", 128 * n, 128 * n + 128)]
+        if e == "v":
+            vs(out, T.Z[:, 0:128], T.hs[:, n:n + 1], None, A.add, None, r, w)
+        else:
+            act(out, T.Z[:, 0:128], F.Identity, r, w, bias=T.hs[:, n:n + 1])
+
+    for n in range(1, NZ):
+        block("a", n)
+
+    def mm_d(q):
+        q.matmul(T.psD[:, 0:129], T.WP[0:16, 1:129], T.X[0:16, 1:130], True, False)
+        q.matmul(T.psD[:, 0:129], T.WM[0:16, 1:129], T.X[0:16, 0:129], False, False)
+        return q.matmul(T.psD[:, 0:129], T.WM[0:16, 0:128], T.X[0:16, 1:130], False, True)
+    op("p", mm_d, [("WP", 0, 144), ("WM", 0, 144), ("X", 0, 130)], [("psD", 0, 512)])
+
+    def mm_e(q):
+        q.matmul(T.psE[:, 0:8], T.AA[:], T.B[:], True, False)
+        return q.matmul(T.psE[:, 1:8], T.Sel[0:8, :], T.cum[0:8, 31:128:16], False, True)
+    op("p", mm_e, [("AA", 0, 128), ("B", 0, 8), ("cum", 16, 144), ("Sel", 0, 128)], [("psE", 0, 512)])
+    act(T.tmp[:, 0:129], T.psD[:, 0:129], F.Identity, [("psD", 0, 512), one("bias")], [("tmp", 0, 129)], bias=col("bias"))
+
+    act(col("wN"), col("w"), F.Copy, [one("w")], [one("wN")], scale=-1.0)
+    act(T.qU[:], T.qV[:], F.Abs, [("qV", 0, 144), one("qg")], [("qU", 0, 144)], bias=col("qg"), scale=-1.0)
+    act(T.T0[:, 0:NL], T.Z[:, 0:NL], F.Copy, [("Z", 0, NL)], [("T0", 0, NL)])
+    act(T.Q[:], T.qU[:], F.Relu, [("qU", 0, 144), one("w"), one("wN")], [("Q", 0, 144)], bias=col("w"), scale=col("wN"))
+    for n in range(NZ, NC // 128):
+        block("v", n)
+
+    vs(T.offs[:], T.psE[:, 0:8], -1.0, None, A.add, None, [("psE", 0, 512)], [("offs", 0, 8)])
+    op("v", lambda q: q.tensor_tensor(T.Z[:, NL:NC].indirect(T.offs[:, 0:8]), T.tmp[:, 1:129], T.Z[:, 0:NT], A.add),
+       [("tmp", 1, 129), ("Z", 0, NT), ("offs", 0, 8)], [("Z", NL, NC)])
+    op("v", lambda q: q.tensor_tensor_scan(T.T0[:, NL:NC], T.Z[:, NL:NC], T.Z[:, NL:NC], T.tmp[:, 0:1], A.add, A.max),
+       [("Z", NL, NC), ("tmp", 0, 1)], [("T0", NL, NC)])
+
+    send(later, "D", NL * rank, NL * rank + NT, "lea", "D", NL * rank, NL * rank + NT)
+
+    wrapped, nbank = {}, [0]
+
+    def wrap(n, lo, hi):
+        tab, b = "T%d" % (n % 2), "psW%d" % (nbank[0] % 4)
+        nbank[0] += 1
+        wrapped[n, lo, hi] = b
+
+        def go(q):
+            for k in range(16):
+                last = q.matmul(T[b][:, 0:(hi - lo) // 16], T.Q[:, 16 - k:144 - k], T[tab][:, NL + lo + k:NL + hi:16], k == 0, k == 15)
+            return last
+        op("p", go, [("Q", 0, 144), (tab, NL + lo, NL + hi)], [(b, 0, 512)])
+
+    def to_list(n, name, lo, hi):
+        if (n, lo, hi) in wrapped:
+            b, c0, c1 = wrapped.pop((n, lo, hi)), lo // 16, hi // 16
+            vs(T[name][:, c0:c1], T[b][:, 0:c1 - c0], -1.0, None, A.mult, None, [(b, 0, 512)], [(name, c0, c1)])
+
+    def gather(e, out, olo, win, wlo, whi, lst, c0, c1):
+        o, i = T[out][:, olo:olo + 16 * (c1 - c0)], T[win][:, wlo:whi].indirect(T[lst][:, c0:c1])
+        r, w = [(win, wlo, whi), (lst, c0, c1)], [(out, olo, olo + 16 * (c1 - c0))]
+        if e == "v":
+            op("v", lambda q: q.tensor_copy(o, i), r, w)
+        else:
+            op("a", lambda q: q.activation(o, i, F.Copy), r, w)
+
+    def both(out, olo, win, wlo, whi, lst, c0, c1):
+        mid = (c0 + c1) // 2
+        gather("v", out, olo, win, wlo, whi, lst, c0, mid)
+        gather("a", out, olo + 16 * (mid - c0), win, wlo, whi, lst, mid, c1)
+
+    def compose(n, lo, hi):
+        m = PLAN[n - 1]
+        to_list(m, "L%d" % (m % 3), lo, hi)
+        both("T%d" % (n % 2), NL + lo, "T%d" % ((n - 1) % 2), 0, NC, "L%d" % (m % 3), lo // 16, hi // 16)
+
+    last = len(PLAN)
+    wrap(0, 0, P)
+    op("v", lambda q: q.memset(T.D[:, NT:NL], 0.0), [], [("D", NT, NL)])
+    op("v", lambda q: q.tensor_copy(T.T1[:, 0:NL], T.Z[:, 0:NL]), [("Z", 0, NL)], [("T1", 0, NL)])
+    for n in range(1, last - 1):
+        compose(n, 0, P)
+        if n in PLAN:
+            wrap(n, 0, P)
+    m = PLAN[last - 2]
+    to_list(m, "L%d" % (m % 3), 0, P)
+    for n in (last - 1, last):
+        for lo, hi in ((W, P), (0, W)):
+            compose(n, lo, hi)
+            wrap(n, lo, hi)
+    to_list(last, "LF", W, P)
+    order = sorted(later, key=lambda c: -T.rank_of(c))
+    for a, b in GROUPS:
+        send(order[a:b], "LF", 32, 64, "m%d" % rank, "M", 32 * rank, 32 * rank + 32)
+    to_list(last, "LF", 0, W)
+
+    for s in range(rank):
+        both("D", NL * (s + 1) + NT, "D", NL * s, NL * s + NL, "M", 32 * s, 32 * s + 32)
+    for h, (lo, hi) in enumerate(((0, CUT), (CUT, P))):
+        both("Y", lo, "D", NL * rank, NL * rank + NL, "LF", lo // 16, hi // 16)
+        dma("s", "st%d" % h, T.y[:, lo:hi], T.Y[:, lo:hi], [("Y", lo, hi)], [])
+    for s in ("qv", "qa", "qp", "qg", "ldln", "ldd0", "ldd1", "ldle"):
+        await_tokens("s", [(s, count[s])])
+    if sent[0]:
+        g.wait_ge(T.sem.sent, sent[0])
+    await_tokens("s", [("st0", 16), ("st1", 16)])

@@ -7,29 +7,31 @@ NC = NL + P
 HALF = 256
 GROUPS = ((0, 2), (2, 4), (4, 7))
 PLAN = (0, 0, 1, 2, 3, 4, 5, 7)
-CUT = 640
-NZ = 10
+CUTS = (0, 640, P)
+FIXED = (("T0", 0, NT), ("T0", NT, HALF), ("T0", HALF, 2 * HALF), ("T0", 2 * HALF, NL),
+         ("T1", 0, HALF), ("T1", HALF, 2 * HALF), ("T1", 2 * HALF, NL))
+ORDER = """rtI qgI lowX p16 sH sL pos posW X0 rt far xb hs topX WP WM Sel lnF psA X bias B F0 Z4 Z1 top Z2 mask cum psD
+AA psE Z3 tmp Z0 HP QS HN offs scatter scan Q F1 F2 F3 F4 F5 F6 zero"""
 
 SCRATCH = {
     "lnI": ("sbuf", [128, 128], "int32"), "dsI": ("sbuf", [128, 128], "int32"),
     "lnF": ("sbuf", [128, 128], "float16"), "cum": ("sbuf", [128, 144], "float16"), "X": ("sbuf", [128, 144], "float16"),
-    "pI": ("sbuf", [128, 8], "int32"), "k7I": ("sbuf", [128, 8], "int32"), "rtI": ("sbuf", [128, 8], "int32"),
-    "qgI": ("sbuf", [128, 8], "int32"),
-    "hN": ("sbuf", [128, 8], "float32"), "lN": ("sbuf", [128, 8], "float32"), "s2": ("sbuf", [128, 8], "float32"),
-    "w1": ("sbuf", [128, 8], "float32"), "w": ("sbuf", [128, 8], "float32"), "wN": ("sbuf", [128, 8], "float32"),
+    "pI": ("sbuf", [128, 8], "int32"), "rtI": ("sbuf", [128, 8], "int32"), "qgI": ("sbuf", [128, 8], "int32"),
+    "sL": ("sbuf", [128, 8], "float32"), "sH": ("sbuf", [128, 8], "float32"), "rt": ("sbuf", [128, 8], "float32"),
+    "pos": ("sbuf", [128, 8], "float32"), "far": ("sbuf", [128, 8], "float32"), "top": ("sbuf", [128, 8], "float32"),
     "lowX": ("sbuf", [128, 8], "float32"), "topX": ("sbuf", [128, 8], "float32"), "bias": ("sbuf", [128, 8], "float32"),
-    "qg": ("sbuf", [128, 8], "float32"), "rt": ("sbuf", [128, 8], "float32"), "pF": ("sbuf", [128, 8], "float32"),
-    "hs": ("sbuf", [128, 16], "float32"),
-    "x1": ("sbuf", [128, 128], "float32"), "c16": ("sbuf", [128, 128], "float32"), "r16": ("sbuf", [128, 128], "float32"),
+    "p16": ("sbuf", [128, 8], "float32"), "posW": ("sbuf", [128, 8], "float32"), "hs": ("sbuf", [128, 8], "float32"),
+    "x": ("sbuf", [128, 256], "bfloat16"), "cS": ("sbuf", [128, 128], "bfloat16"), "r16": ("sbuf", [128, 128], "bfloat16"),
     "Sel": ("sbuf", [128, 128], "float16"), "mask": ("sbuf", [128, 128], "bfloat16"), "B": ("sbuf", [128, 8], "float16"),
     "AA": ("sbuf", [128, 128], "float16"),
-    "wV": ("sbuf", [128, 144], "float32"), "WP": ("sbuf", [128, 144], "float16"), "WM": ("sbuf", [128, 144], "float16"),
-    "qV": ("sbuf", [128, 144], "float32"), "qU": ("sbuf", [128, 144], "float32"), "Q": ("sbuf", [128, 144], "bfloat16"),
+    "WP": ("sbuf", [128, 144], "float16"), "WM": ("sbuf", [128, 144], "float16"),
+    "QS": ("sbuf", [128, 144], "bfloat16"), "Q": ("sbuf", [128, 144], "bfloat16"),
+    "HP": ("sbuf", [128, 144], "bfloat16"), "HN": ("sbuf", [128, 144], "bfloat16"),
     "tmp": ("sbuf", [128, 144], "bfloat16"), "offs": ("sbuf", [128, 8], "uint16"),
-    "Z": ("sbuf", [128, NC], "bfloat16"),
-    "T0": ("sbuf", [128, NC], "bfloat16"), "T1": ("sbuf", [128, NC], "bfloat16"),
+    "Z": ("sbuf", [128, P], "bfloat16"),
+    "T0": ("sbuf", [128, NC], "bfloat16"), "T1": ("sbuf", [128, NC], "bfloat16"), "U": ("sbuf", [128, W], "bfloat16"),
     "L0": ("sbuf", [128, 64], "uint16"), "L1": ("sbuf", [128, 64], "uint16"), "L2": ("sbuf", [128, 64], "uint16"),
-    "LF": ("sbuf", [128, 64], "uint16"),
+    "LF": ("sbuf", [128, 64], "uint16"), "LT": ("sbuf", [128, 32], "uint16"), "LM": ("sbuf", [128, 32], "uint16"),
     "M": ("sbuf", [128, 256], "uint16"),
     "D": ("sbuf", [128, 8 * NL], "bfloat16"),
     "Y": ("sbuf", [128, P], "bfloat16"),
@@ -37,7 +39,8 @@ SCRATCH = {
     "psW0": ("psum", [128, 512], "float32"), "psW1": ("psum", [128, 512], "float32"), "psW2": ("psum", [128, 512], "float32"),
     "psW3": ("psum", [128, 512], "float32"),
 }
-SEMAPHORES = ["qv", "qa", "qp", "qg", "ldln", "ldd0", "ldd1", "ldle", "st0", "st1", "lea", "sent"] + ["m%d" % s for s in range(8)]
+SEMAPHORES = ["qv", "qa", "qp", "qg", "ldln", "ldd0", "ldd1", "ldle", "lea", "sent"] + ["m%d" % s for s in range(8)] + [
+    "st%d" % s for s in range(len(CUTS) - 1)]
 
 
 def rank_program(g, core, T, topo):
@@ -89,6 +92,14 @@ def rank_program(g, core, T, topo):
         call(queue[e]).then_inc(T.sem[s], 1)
         record(e, (s, count[s]), reads, writes)
 
+    def sums(bank, calls):
+        for n, (out, lhsT, rhs, reads) in enumerate(calls):
+            depend("p", reads, [] if n else [(bank, 0, 512)])
+            last = g.tensor.matmul(out, lhsT, rhs, n == 0, n == len(calls) - 1)
+        count["qp"] = count.get("qp", 0) + 1
+        last.then_inc(T.sem.qp, 1)
+        record("p", ("qp", count["qp"]), [r for c in calls for r in c[3]], [(bank, 0, 512)])
+
     def dma(e, sem, out, in_, reads, writes):
         depend(e, reads, writes)
         count[sem] = count.get(sem, 0) + 16
@@ -97,6 +108,7 @@ def rank_program(g, core, T, topo):
 
     later = [c for c in T.cores if T.rank_of(c) > rank]
     sent = [0]
+    top = len(T.cores) - 1
 
     def lanes(src, dst):
         if topo.chip(src) != topo.chip(dst):
@@ -134,26 +146,31 @@ def rank_program(g, core, T, topo):
         record(None, ("lea", sum(len(lanes(T.cores[s], core)) for s in range(rank))), [],
                [("D", NL * s, NL * s + NT) for s in range(rank)])
         for s in range(rank):
-            record(None, ("m%d" % s, len(lanes(T.cores[s], core))), [], [("M", 32 * s, 32 * s + 32)])
+            if rank == top and s == top - 2:
+                continue
+            by = s - 1 if s == top - 1 else s
+            record(None, ("m%d" % s, len(lanes(T.cores[by], core))), [], [("M", 32 * s, 32 * s + 32)])
+    if rank == top - 2:
+        record(None, ("m%d" % top, len(lanes(T.cores[top - 1], core))), [], [("M", 32 * top, 32 * top + 32)])
 
     dma("s", "ldln", T.lnI[0:8, :], T.ln[:], [], [("lnI", 0, 128)])
-    dma("a", "ldd0", T.dsI[0:8, :], T.ds[:], [], [("dsI", 0, 64)])
+    dma("a", "ldle", T.D[:, NL * rank:NL * rank + NT], T.le[:], [], [("D", NL * rank, NL * rank + NT)])
+    dma("s", "ldd0", T.dsI[0:8, :], T.ds[:], [], [("dsI", 0, 64)])
     dma("s", "ldd1", T.dsI[8:16, :], T.ds[:], [], [("dsI", 64, 128)])
-    dma("s", "ldle", T.D[:, NL * rank:NL * rank + NT], T.le[:], [], [("D", NL * rank, NL * rank + NT)])
 
-    def iota(name, rows, n, pattern, base, cm):
+    def iota(name, rows, n, pattern, cm):
         out = T[name][0:rows, 0:n]
         if name == "pI":
-            op("g", lambda q: q.iota(out, pattern, base, cm), [], [(name, 0, n)])
+            op("g", lambda q: q.iota(out, pattern, 0, cm), [], [(name, 0, n)])
         else:
-            op("g", lambda q: q.iota(out, pattern, base, cm, allow_small_or_imprecise_dtypes=True), [], [(name, 0, n)])
+            op("g", lambda q: q.iota(out, pattern, 0, cm, allow_small_or_imprecise_dtypes=True), [], [(name, 0, n)])
 
-    iota("pI", 128, 2, [[0, 2]], 0, 1)
-    iota("c16", 128, 128, [[1, 8], [0, 16]], 0, 0)
-    iota("x1", 128, 128, [[1, 128]], 0, 0)
-    iota("r16", 128, 128, [[0, 8], [1, 16]], 0, 0)
-    iota("wV", 16, 144, [[1, 9], [8, 2], [100, 8]], -100, -1)
-    iota("qV", 128, 144, [[1, 9], [1000, 16]], -1, 0)
+    iota("pI", 128, 2, [[0, 2]], 1)
+    iota("x", 128, 144, [[1, 144]], 0)
+    iota("cS", 8, 128, [[1, 8], [0, 16]], -1)
+    iota("r16", 128, 128, [[0, 8], [1, 16]], 0)
+
+    send(later, "D", NL * rank, NL * rank + NT, "lea", "D", NL * rank, NL * rank + NT)
 
     def vs(out, in0, s1, s2, op0, op1, reads, writes):
         if op1 is None:
@@ -164,106 +181,124 @@ def rank_program(g, core, T, topo):
     def act(out, in_, func, reads, writes, bias=0.0, scale=1.0):
         op("a", lambda q: q.activation(out, in_, func, bias=bias, scale=scale), reads, writes)
 
-    def col(name):
-        return T[name][:, 0:1]
+    def col(name, rows=128):
+        return T[name][0:rows, 0:1]
 
     def one(name):
         return (name, 0, 1)
 
-    def copy_col(name, src):
-        op("v", lambda q: q.tensor_copy(col(name), col(src)), [one(src)], [one(name)])
+    def vcol(name, src, s1, s2, op0, op1):
+        vs(col(name), col(src), s1, s2, op0, op1, [one(src)], [one(name)])
 
-    vs(col("k7I"), col("pI"), 7, None, A.bitwise_and, None, [one("pI")], [one("k7I")])
-    vs(col("rtI"), col("pI"), 15, None, A.bitwise_and, None, [one("pI")], [one("rtI")])
-    vs(col("qgI"), col("pI"), 4, None, A.arith_shift_right, None, [one("pI")], [one("qgI")])
-    vs(T.lowX[0:16, 0:2], T.pI[0:16, 0:2], 8.0, float(HALF), A.is_lt, A.mult, [("pI", 0, 2)], [("lowX", 0, 2)])
-    copy_col("pF", "pI")
-    act(T.topX[0:16, 0:1], T.lowX[0:16, 0:1], F.Copy, [one("lowX")], [one("topX")], bias=float(HALF))
-    vs(col("hN"), col("k7I"), 2.0, -1.0, A.is_equal, A.mult, [one("k7I")], [one("hN")])
-    vs(col("lN"), col("k7I"), 3.0, -1.0, A.is_equal, A.mult, [one("k7I")], [one("lN")])
-    vs(col("s2"), col("k7I"), 2.0, None, A.is_lt, None, [one("k7I")], [one("s2")])
-    op("v", lambda q: q.tensor_copy(T.X[0:16, 0:130:129], T.lowX[0:16, 0:2]), [("lowX", 0, 2)], [("X", 0, 1), ("X", 129, 130)])
-    copy_col("rt", "rtI")
-    copy_col("qg", "qgI")
-    vs(T.Sel[0:8, :], T.c16[0:8, :], T.pF[0:8, 0:1], None, A.is_equal, None, [("c16", 0, 128), one("pF")], [("Sel", 0, 128)])
-    vs(T.B[:], T.c16[:, 0:128:16], col("qg"), None, A.is_equal, None, [("c16", 0, 128), one("qg")], [("B", 0, 8)])
-    vs(col("bias"), col("rtI"), 1.0, float(HALF), A.is_equal, A.mult, [one("rtI")], [one("bias")])
-    vs(T.mask[:], T.r16[:], col("rt"), None, A.is_ge, None, [("r16", 0, 128), one("rt")], [("mask", 0, 128)])
+    def block(name, first, lo, hi):
+        n = lo // HALF
+        act(T[name][:, lo - first:hi - first], T.x[:, lo - n * HALF:hi - n * HALF], F.Identity,
+            [("x", lo - n * HALF, hi - n * HALF), one("sL"), ("hs", n, n + 1)], [(name, lo - first, hi - first)],
+            bias=T.hs[:, n:n + 1], scale=col("sL"))
 
-    vs(T.lnF[0:8, :], T.lnI[0:8, :], 1.0, None, A.add, None, [("lnI", 0, 128)], [("lnF", 0, 128)])
-    op("p", lambda q: q.matmul(T.psA[:, 0:128], T.lnF[0:8, :], T.Sel[0:8, :], True, True),
-       [("lnF", 0, 128), ("Sel", 0, 128)], [("psA", 0, 512)])
-    vs(T.X[0:16, 1:129], T.dsI[0:16, :], T.lowX[0:16, 0:1], T.topX[0:16, 0:1], A.max, A.min,
-       [("dsI", 0, 128), one("lowX"), one("topX")], [("X", 1, 129)])
-    for name, c in (("WP", 1.0), ("WM", -1.0)):
-        vs(T[name][0:16, :], T.wV[0:16, :], 0.0, c, A.is_equal, A.mult, [("wV", 0, 144)], [(name, 0, 144)])
-    op("v", lambda q: q.tensor_tensor_scan(T.cum[0:8, 16:144], T.lnF[0:8, :], T.lnF[0:8, :], 0.0, A.add, A.max),
-       [("lnF", 0, 128)], [("cum", 16, 144)])
-    op("v", lambda q: q.tensor_tensor(T.AA[:], T.psA[:, 0:128], T.mask[:], A.mult),
-       [("psA", 0, 512), ("mask", 0, 128)], [("AA", 0, 128)])
+    def from_x(name, rows, cols, s1, s2, op0, op1):
+        n, named = len(range(144)[cols]), isinstance(s2, str)
+        vs(T[name][0:rows, 0:n], T.x[0:rows, cols], col(s1, rows), col(s2, rows) if named else s2, op0, op1,
+           [("x", 0, 144), one(s1)] + ([one(s2)] if named else []), [(name, 0, n)])
 
-    act(col("w1"), col("hN"), F.Identity, [one("hN"), one("s2")], [one("w1")], bias=col("s2"), scale=-64.0)
-    act(T.hs[:, 0:13], T.x1[:, 0:13], F.Copy, [("x1", 0, 13), one("hN")], [("hs", 0, 13)], scale=col("hN"))
-    act(T.Z[:, 0:128], T.x1[:], F.Copy, [("x1", 0, 128), one("lN")], [("Z", 0, 128)], scale=col("lN"))
-    act(col("w"), col("lN"), F.Identity, [one("lN"), one("w1")], [one("w")], bias=col("w1"), scale=-0.5)
+    def zero():
+        for lo in range(NT, NL, HALF):
+            act(T.D[:, lo:lo + HALF], T.x[:], F.Copy, [("x", 0, HALF)], [("D", lo, lo + HALF)], scale=0.0)
 
-    def block(e, n):
-        out, r, w = T.Z[:, 128 * n:128 * n + 128], [("Z", 0, 128), ("hs", n, n + 1)], [("Z", 128 * n, 128 * n + 128)]
-        if e == "v":
-            vs(out, T.Z[:, 0:128], T.hs[:, n:n + 1], None, A.add, None, r, w)
-        else:
-            act(out, T.Z[:, 0:128], F.Identity, r, w, bias=T.hs[:, n:n + 1])
-
-    for n in range(1, NZ):
-        block("a", n)
-
-    def mm_d(q):
-        q.matmul(T.psD[:, 0:129], T.WP[0:16, 1:129], T.X[0:16, 1:130], True, False)
-        q.matmul(T.psD[:, 0:129], T.WM[0:16, 1:129], T.X[0:16, 0:129], False, False)
-        return q.matmul(T.psD[:, 0:129], T.WM[0:16, 0:128], T.X[0:16, 1:130], False, True)
-    op("p", mm_d, [("WP", 0, 144), ("WM", 0, 144), ("X", 0, 130)], [("psD", 0, 512)])
-
-    def mm_e(q):
-        q.matmul(T.psE[:, 0:8], T.AA[:], T.B[:], True, False)
-        return q.matmul(T.psE[:, 1:8], T.Sel[0:8, :], T.cum[0:8, 31:128:16], False, True)
-    op("p", mm_e, [("AA", 0, 128), ("B", 0, 8), ("cum", 16, 144), ("Sel", 0, 128)], [("psE", 0, 512)])
-    act(T.tmp[:, 0:129], T.psD[:, 0:129], F.Identity, [("psD", 0, 512), one("bias")], [("tmp", 0, 129)], bias=col("bias"))
-
-    act(col("wN"), col("w"), F.Copy, [one("w")], [one("wN")], scale=-1.0)
-    act(T.qU[:], T.qV[:], F.Abs, [("qV", 0, 144), one("qg")], [("qU", 0, 144)], bias=col("qg"), scale=-1.0)
-    act(T.T0[:, 0:NL], T.Z[:, 0:NL], F.Copy, [("Z", 0, NL)], [("T0", 0, NL)])
-    act(T.Q[:], T.qU[:], F.Relu, [("qU", 0, 144), one("w"), one("wN")], [("Q", 0, 144)], bias=col("w"), scale=col("wN"))
-    for n in range(NZ, NC // 128):
-        block("v", n)
-
-    vs(T.offs[:], T.psE[:, 0:8], -1.0, None, A.add, None, [("psE", 0, 512)], [("offs", 0, 8)])
-    op("v", lambda q: q.tensor_tensor(T.Z[:, NL:NC].indirect(T.offs[:, 0:8]), T.tmp[:, 1:129], T.Z[:, 0:NT], A.add),
-       [("tmp", 1, 129), ("Z", 0, NT), ("offs", 0, 8)], [("Z", NL, NC)])
-    op("v", lambda q: q.tensor_tensor_scan(T.T0[:, NL:NC], T.Z[:, NL:NC], T.Z[:, NL:NC], T.tmp[:, 0:1], A.add, A.max),
-       [("Z", NL, NC), ("tmp", 0, 1)], [("T0", NL, NC)])
-
-    send(later, "D", NL * rank, NL * rank + NT, "lea", "D", NL * rank, NL * rank + NT)
+    wide = slice(0, 144)
+    rd = [("WP", 0, 144), ("WM", 0, 144), ("X", 0, 130)]
+    zcut = [NL] + list(range(3 * HALF, NC, HALF)) + [NC]
+    step = {
+        "rtI": lambda: vcol("rtI", "pI", 15, None, A.bitwise_and, None),
+        "qgI": lambda: vcol("qgI", "pI", 4, None, A.arith_shift_right, None),
+        "lowX": lambda: vs(T.lowX[0:16, 0:2], T.pI[0:16, 0:2], 8.0, float(HALF), A.is_lt, A.mult, [("pI", 0, 2)], [("lowX", 0, 2)]),
+        "p16": lambda: vcol("p16", "pI", 16.0, -125.0, A.mult, A.add),
+        "sH": lambda: vcol("sH", "rtI", 4.0, -float(HALF), A.is_equal, A.mult),
+        "sL": lambda: vcol("sL", "rtI", 5.0, -1.0, A.is_equal, A.mult),
+        "pos": lambda: vcol("pos", "qgI", 16.0, 16.0, A.mult, A.add),
+        "far": lambda: vcol("far", "rtI", 2.0, 1000.0, A.is_ge, A.mult),
+        "rt": lambda: vcol("rt", "rtI", 0.0, None, A.add, None),
+        "bias": lambda: vcol("bias", "rtI", 2.0, float(HALF), A.is_equal, A.mult),
+        "posW": lambda: vs(col("posW", 16), col("lowX", 16), 127.0 / HALF, col("p16", 16), A.mult, A.add,
+                           [one("lowX"), one("p16")], [one("posW")]),
+        "X0": lambda: op("v", lambda q: q.tensor_copy(T.X[0:16, 0:130:129], T.lowX[0:16, 0:2]), [("lowX", 0, 2)],
+                         [("X", 0, 1), ("X", 129, 130)]),
+        "topX": lambda: act(col("topX", 16), col("lowX", 16), F.Copy, [one("lowX")], [one("topX")], bias=float(HALF)),
+        "hs": lambda: act(T.hs[:, 0:8], T.x[:, 0:8], F.Copy, [("x", 0, 8), one("sH")], [("hs", 0, 8)], scale=col("sH")),
+        "top": lambda: act(col("top"), col("far"), F.Identity, [one("far"), one("pos")], [one("top")], bias=col("pos")),
+        "B": lambda: from_x("B", 128, slice(16, 144, 16), "pos", None, A.is_equal, None),
+        "WP": lambda: from_x("WP", 16, wide, "posW", 1.0, A.is_equal, A.mult),
+        "WM": lambda: from_x("WM", 16, wide, "posW", -1.0, A.is_equal, A.mult),
+        "HP": lambda: from_x("HP", 128, wide, "top", None, A.is_ge, None),
+        "HN": lambda: from_x("HN", 128, wide, "top", -1.0, A.is_ge, A.mult),
+        "QS": lambda: from_x("QS", 128, wide, "top", "pos", A.min, A.is_equal),
+        "Q": lambda: from_x("Q", 128, wide, "pos", None, A.is_equal, None),
+        "Sel": lambda: vs(T.Sel[0:8, :], T.cS[0:8, :], 0.0, None, A.is_equal, None, [("cS", 0, 128)], [("Sel", 0, 128)]),
+        "mask": lambda: vs(T.mask[:], T.r16[:], col("rt"), None, A.is_ge, None, [("r16", 0, 128), one("rt")], [("mask", 0, 128)]),
+        "lnF": lambda: vs(T.lnF[0:8, :], T.lnI[0:8, :], 1.0, None, A.add, None, [("lnI", 0, 128)], [("lnF", 0, 128)]),
+        "psA": lambda: sums("psA", [(T.psA[:, 0:128], T.lnF[0:8, :], T.Sel[0:8, :], [("lnF", 0, 128), ("Sel", 0, 128)])]),
+        "AA": lambda: op("v", lambda q: q.tensor_tensor(T.AA[:], T.psA[:, 0:128], T.mask[:], A.mult),
+                         [("psA", 0, 512), ("mask", 0, 128)], [("AA", 0, 128)]),
+        "cum": lambda: op("v", lambda q: q.tensor_tensor_scan(T.cum[0:8, 16:144], T.lnF[0:8, :], T.lnF[0:8, :], 0.0, A.add, A.max),
+                          [("lnF", 0, 128)], [("cum", 16, 144)]),
+        "psE": lambda: sums("psE", [(T.psE[:, 0:8], T.AA[:], T.B[:], [("AA", 0, 128), ("B", 0, 8)]),
+                                    (T.psE[:, 1:8], T.Sel[0:8, :], T.cum[0:8, 31:128:16], [("cum", 16, 144), ("Sel", 0, 128)])]),
+        "offs": lambda: vs(T.offs[:], T.psE[:, 0:8], -1.0, None, A.add, None, [("psE", 0, 512)], [("offs", 0, 8)]),
+        "X": lambda: vs(T.X[0:16, 1:129], T.dsI[0:16, :], col("lowX", 16), col("topX", 16), A.max, A.min,
+                        [("dsI", 0, 128), one("lowX"), one("topX")], [("X", 1, 129)]),
+        "psD": lambda: sums("psD", [(T.psD[:, 0:129], T.WP[0:16, 2:130], T.X[0:16, 1:130], rd),
+                                    (T.psD[:, 0:129], T.WM[0:16, 2:130], T.X[0:16, 0:129], rd),
+                                    (T.psD[:, 0:129], T.WM[0:16, 0:128], T.X[0:16, 1:130], rd)]),
+        "tmp": lambda: act(T.tmp[:, 0:129], T.psD[:, 0:129], F.Identity, [("psD", 0, 512), one("bias")], [("tmp", 0, 129)],
+                           bias=col("bias")),
+        "scatter": lambda: op("v", lambda q: q.tensor_tensor(T.Z[:, 0:P].indirect(T.offs[:, 0:8]), T.tmp[:, 1:129], T.T0[:, 0:NT], A.add),
+                              [("tmp", 1, 129), ("T0", 0, NT), ("offs", 0, 8)], [("Z", 0, P)]),
+        "scan": lambda: op("v", lambda q: q.tensor_tensor_scan(T.T0[:, NL:NC], T.Z[:], T.Z[:], T.tmp[:, 0:1], A.add, A.max),
+                           [("Z", 0, P), ("tmp", 0, 1)], [("T0", NL, NC)]),
+        "zero": zero,
+        "xb": lambda: act(T.x[:, 144:HALF], T.x[:, 0:HALF - 144], F.Copy, [("x", 0, 144)], [("x", 144, HALF)], bias=144.0),
+    }
+    for n in range(len(zcut) - 1):
+        step["Z%d" % n] = lambda n=n: block("Z", NL, zcut[n], zcut[n + 1])
+    for n, (name, lo, hi) in enumerate(FIXED):
+        step["F%d" % n] = lambda a=(name, 0, lo, hi): block(*a)
+    for name in ORDER.split():
+        step[name]()
 
     wrapped, nbank = {}, [0]
 
-    def wrap(n, lo, hi):
-        tab, b = "T%d" % (n % 2), "psW%d" % (nbank[0] % 4)
+    def bank():
         nbank[0] += 1
-        wrapped[n, lo, hi] = b
+        return "psW%d" % (nbank[0] % 4)
 
-        def go(q):
-            for k in range(16):
-                last = q.matmul(T[b][:, 0:(hi - lo) // 16], T.Q[:, 16 - k:144 - k], T[tab][:, NL + lo + k:NL + hi:16], k == 0, k == 15)
-            return last
-        op("p", go, [("Q", 0, 144), (tab, NL + lo, NL + hi)], [(b, 0, 512)])
+    def wrap_first():
+        b = wrapped[0] = bank()
+        rz, rt = [("QS", 0, 144), ("Z", 0, P)], [("HP", 0, 144), ("HN", 0, 144), ("T0", NL, NC)]
+        sums(b, [(T[b][:, 0:64], T.QS[:, 16 - k:144 - k], T.Z[:, k:P:16], rz) for k in range(16)]
+             + [(T[b][:, 0:1], T.HP[:, 16:144], T.tmp[:, 0:1], [("HP", 0, 144), ("tmp", 0, 1)]),
+                (T[b][:, 1:64], T.HP[:, 16:144], T.T0[:, NL + 15:NC - 16:16], rt),
+                (T[b][:, 0:64], T.HN[:, 0:128], T.T0[:, NL + 15:NC:16], rt)])
 
-    def to_list(n, name, lo, hi):
-        if (n, lo, hi) in wrapped:
-            b, c0, c1 = wrapped.pop((n, lo, hi)), lo // 16, hi // 16
-            vs(T[name][:, c0:c1], T[b][:, 0:c1 - c0], -1.0, None, A.mult, None, [(b, 0, 512)], [(name, c0, c1)])
+    def wrap(n, tab=None, lo=NL, hi=NC):
+        tab, b = tab or "T%d" % (n % 2), bank()
+        wrapped[n] = b
+        r = [("Q", 0, 144), (tab, lo, hi)]
+        sums(b, [(T[b][:, 0:(hi - lo) // 16], T.Q[:, 16 - k:144 - k], T[tab][:, lo + k:hi:16], r) for k in range(16)])
 
-    def gather(e, out, olo, win, wlo, whi, lst, c0, c1):
-        o, i = T[out][:, olo:olo + 16 * (c1 - c0)], T[win][:, wlo:whi].indirect(T[lst][:, c0:c1])
+    def turn(key, tab, first):
+        b = wrapped[key] = bank()
+        sums(b, [(T[b][:, 0:32], T.Q[:, 16 - k:144 - k], T[tab][:, first + 32 * k:first + 32 * k + 32],
+                  [("Q", 0, 144), (tab, first + 32 * k, first + 32 * k + 32)]) for k in range(16)])
+
+    def to_list(key, name, n=64):
+        if key in wrapped:
+            b = wrapped.pop(key)
+            vs(T[name][:, 0:n], T[b][:, 0:n], -1.0, None, A.mult, None, [(b, 0, 512)], [(name, 0, n)])
+
+    def gather(e, out, olo, win, wlo, whi, lst, c0, c1, o=None):
+        i = T[win][:, wlo:whi].indirect(T[lst][:, c0:c1])
+        if o is None:
+            o = T[out][:, olo:olo + 16 * (c1 - c0)]
         r, w = [(win, wlo, whi), (lst, c0, c1)], [(out, olo, olo + 16 * (c1 - c0))]
         if e == "v":
             op("v", lambda q: q.tensor_copy(o, i), r, w)
@@ -277,36 +312,73 @@ def rank_program(g, core, T, topo):
 
     def compose(n, lo, hi):
         m = PLAN[n - 1]
-        to_list(m, "L%d" % (m % 3), lo, hi)
+        to_list(m, "L%d" % (m % 3))
         both("T%d" % (n % 2), NL + lo, "T%d" % ((n - 1) % 2), 0, NC, "L%d" % (m % 3), lo // 16, hi // 16)
 
     last = len(PLAN)
-    wrap(0, 0, P)
-    op("v", lambda q: q.memset(T.D[:, NT:NL], 0.0), [], [("D", NT, NL)])
-    op("v", lambda q: q.tensor_copy(T.T1[:, 0:NL], T.Z[:, 0:NL]), [("Z", 0, NL)], [("T1", 0, NL)])
+    wrap_first()
     for n in range(1, last - 1):
         compose(n, 0, P)
         if n in PLAN:
-            wrap(n, 0, P)
-    m = PLAN[last - 2]
-    to_list(m, "L%d" % (m % 3), 0, P)
-    for n in (last - 1, last):
-        for lo, hi in ((W, P), (0, W)):
-            compose(n, lo, hi)
-            wrap(n, lo, hi)
-    to_list(last, "LF", W, P)
-    order = sorted(later, key=lambda c: -T.rank_of(c))
-    for a, b in GROUPS:
-        send(order[a:b], "LF", 32, 64, "m%d" % rank, "M", 32 * rank, 32 * rank + 32)
-    to_list(last, "LF", 0, W)
+            wrap(n)
+    tab = "T%d" % ((last - 1) % 2)
+    if later:
+        for lo in (W, W + W // 2):
+            compose(last - 1, lo, lo + W // 2)
+        turn("t", tab, NL + W)
+        compose(last - 1, 0, W)
+        to_list("t", "LT", 32)
+        for c in (0, 16):
+            both("U", 16 * c, tab, 0, NC, "LT", c, c + 16)
+        turn("m", "U", 0)
+        to_list("m", "LM", 32)
+        order = sorted(later, key=lambda c: -T.rank_of(c))
+        slot = rank
+        if rank == top - 2:
+            order = order[1:]
+        if rank == top - 1:
+            order, slot = [T.cores[top - 2]], top
+        for a, b in GROUPS:
+            send(order[a:b], "LM", 0, 32, "m%d" % slot, "M", 32 * slot, 32 * slot + 32)
+    else:
+        compose(last - 1, 0, P)
+    wrap(last - 1)
+    if rank != top - 2:
+        compose(last, 0, P)
+        wrap(last)
+    else:
+        block("T0", 2 * NL - NC, NL, NL + NT)
+        to_list(last - 1, "L1")
+        gather("v", "T0", NL - NT, tab, 0, NC, "L1", 0, 32)
+        gather("a", "T0", NL + W, tab, 0, NC, "L1", 32, 64)
+        both("U", 0, "T0", NC - NL, NC, "M", 32 * top, 32 * top + 32)
+        wrap("p", "U", 0, W)
+        wrap(last, "T0", NL - NT, NC)
 
     for s in range(rank):
-        both("D", NL * (s + 1) + NT, "D", NL * s, NL * s + NL, "M", 32 * s, 32 * s + 32)
-    for h, (lo, hi) in enumerate(((0, CUT), (CUT, P))):
+        at, lo, hi = NL * (s + 1) + NT, NL * s, NL * s + NL
+        if rank == top and s == top - 2:
+            continue
+        if s == top - 1:
+            lo, hi = lo - NL, lo + NT
+        for h, e in enumerate("va"):
+            gather(e, "D", at + h * W // 2, "D", lo, hi, "M", 32 * s + 16 * h, 32 * s + 16 * h + 16,
+                   T.D[:, at + h:at + W:2])
+        if rank != top - 2:
+            to_list(last, "LF")
+        elif s == 0:
+            to_list("p", "LT", 32)
+            send([T.cores[top]], "LT", 0, 32, "m%d" % (top - 1), "M", 32 * (top - 1), 32 * top)
+        elif s == 1:
+            b = wrapped.pop(last)
+            for c, d in ((0, 0), (32, 40)):
+                vs(T.LF[:, c:c + 32], T[b][:, d:d + 32], -1.0, None, A.mult, None, [(b, 0, 512)], [("LF", c, c + 32)])
+    to_list(last, "LF")
+    for h, (lo, hi) in enumerate(zip(CUTS, CUTS[1:])):
         both("Y", lo, "D", NL * rank, NL * rank + NL, "LF", lo // 16, hi // 16)
         dma("s", "st%d" % h, T.y[:, lo:hi], T.Y[:, lo:hi], [("Y", lo, hi)], [])
     for s in ("qv", "qa", "qp", "qg", "ldln", "ldd0", "ldd1", "ldle"):
         await_tokens("s", [(s, count[s])])
     if sent[0]:
         g.wait_ge(T.sem.sent, sent[0])
-    await_tokens("s", [("st0", 16), ("st1", 16)])
+    await_tokens("s", [("st%d" % h, 16) for h in range(len(CUTS) - 1)])

from concourse.bass import DstId, RemoteDMATransfer
from concourse.mybir import AluOpType, ActivationFunctionType

P, NT, W = 1024, 128, 512
NL = NT + W
NC = NL + P
HALF = 256
GROUPS = ((0, 2), (2, 4), (4, 7))
PLAN = (0, 0, 1, 2, 3, 4, 5, 7)
CUTS = (0, 640, P)
FIXED = (("T0", 0, NT), ("T0", NT, HALF), ("T0", HALF, 2 * HALF), ("T0", 2 * HALF, NL),
         ("T1", 0, HALF), ("T1", HALF, 2 * HALF), ("T1", 2 * HALF, NL))
ORDER = """rtI qgI lowX p16 sH sL pos posW X0 rt far xb hs topX WP WM Sel lnF psA X bias B F0 Z4 Z1 top Z2 mask cum psD
AA psE Z3 tmp Z0 HP QS HN offs scatter scan Q F1 F2 F3 F4 F5 F6 zero"""

SCRATCH = {
    "lnI": ("sbuf", [128, 128], "int32"), "dsI": ("sbuf", [128, 128], "int32"),
    "lnF": ("sbuf", [128, 128], "float16"), "cum": ("sbuf", [128, 144], "float16"), "X": ("sbuf", [128, 144], "float16"),
    "pI": ("sbuf", [128, 8], "int32"), "rtI": ("sbuf", [128, 8], "int32"), "qgI": ("sbuf", [128, 8], "int32"),
    "sL": ("sbuf", [128, 8], "float32"), "sH": ("sbuf", [128, 8], "float32"), "rt": ("sbuf", [128, 8], "float32"),
    "pos": ("sbuf", [128, 8], "float32"), "far": ("sbuf", [128, 8], "float32"), "top": ("sbuf", [128, 8], "float32"),
    "lowX": ("sbuf", [128, 8], "float32"), "topX": ("sbuf", [128, 8], "float32"), "bias": ("sbuf", [128, 8], "float32"),
    "p16": ("sbuf", [128, 8], "float32"), "posW": ("sbuf", [128, 8], "float32"), "hs": ("sbuf", [128, 8], "float32"),
    "x": ("sbuf", [128, 256], "bfloat16"), "cS": ("sbuf", [128, 128], "bfloat16"), "r16": ("sbuf", [128, 128], "bfloat16"),
    "Sel": ("sbuf", [128, 128], "float16"), "mask": ("sbuf", [128, 128], "bfloat16"), "B": ("sbuf", [128, 8], "float16"),
    "AA": ("sbuf", [128, 128], "float16"),
    "WP": ("sbuf", [128, 144], "float16"), "WM": ("sbuf", [128, 144], "float16"),
    "QS": ("sbuf", [128, 144], "bfloat16"), "Q": ("sbuf", [128, 144], "bfloat16"),
    "HP": ("sbuf", [128, 144], "bfloat16"), "HN": ("sbuf", [128, 144], "bfloat16"),
    "tmp": ("sbuf", [128, 144], "bfloat16"), "offs": ("sbuf", [128, 8], "uint16"),
    "Z": ("sbuf", [128, P], "bfloat16"),
    "T0": ("sbuf", [128, NC], "bfloat16"), "T1": ("sbuf", [128, NC], "bfloat16"), "U": ("sbuf", [128, W], "bfloat16"),
    "L0": ("sbuf", [128, 64], "uint16"), "L1": ("sbuf", [128, 64], "uint16"), "L2": ("sbuf", [128, 64], "uint16"),
    "LF": ("sbuf", [128, 64], "uint16"), "LT": ("sbuf", [128, 32], "uint16"), "LM": ("sbuf", [128, 32], "uint16"),
    "M": ("sbuf", [128, 256], "uint16"),
    "D": ("sbuf", [128, 8 * NL], "bfloat16"),
    "Y": ("sbuf", [128, P], "bfloat16"),
    "psA": ("psum", [128, 512], "float32"), "psE": ("psum", [128, 512], "float32"), "psD": ("psum", [128, 512], "float32"),
    "psW0": ("psum", [128, 512], "float32"), "psW1": ("psum", [128, 512], "float32"), "psW2": ("psum", [128, 512], "float32"),
    "psW3": ("psum", [128, 512], "float32"),
}
SEMAPHORES = ["qv", "qa", "qp", "qg", "ldln", "ldd0", "ldd1", "ldle", "lea", "sent"] + ["m%d" % s for s in range(8)] + [
    "st%d" % s for s in range(len(CUTS) - 1)]


def rank_program(g, core, T, topo):
    rank = T.rank_of(core)
    if rank is None:
        return
    queue = {"v": g.vector, "a": g.scalar, "p": g.tensor, "g": g, "s": g.sync}
    known = {e: {} for e in queue}
    snap = {}
    count = {}
    acc = {}

    def await_tokens(e, toks):
        best = {}
        for s, v in toks:
            if known[e].get(s, 0) < v:
                best[s] = max(best.get(s, 0), v)
        for s, v in sorted(best.items()):
            if any(t != s and snap.get((t, best[t]), {}).get(s, 0) >= v for t in best):
                continue
            if known[e].get(s, 0) >= v:
                continue
            queue[e].wait_ge(T.sem[s], v)
            known[e][s] = v
            for t, w in snap.get((s, v), {}).items():
                known[e][t] = max(known[e].get(t, 0), w)

    def depend(e, reads, writes):
        toks = []
        for b, lo, hi in reads:
            toks += [a[3] for a in acc.get(b, []) if a[2] and a[0] < hi and lo < a[1]]
        for b, lo, hi in writes:
            toks += [a[3] for a in acc.get(b, []) if a[0] < hi and lo < a[1]]
        await_tokens(e, toks)

    def record(e, tok, reads, writes):
        if e is not None:
            snap[tok] = dict(known[e])
            snap[tok][tok[0]] = tok[1]
        for b, lo, hi in writes:
            acc[b] = [a for a in acc.get(b, []) if not (lo <= a[0] and a[1] <= hi)] + [[lo, hi, True, tok]]
        for b, lo, hi in reads:
            acc.setdefault(b, []).append([lo, hi, False, tok])

    def op(e, call, reads, writes):
        depend(e, reads, writes)
        s = "q" + e
        count[s] = count.get(s, 0) + 1
        call(queue[e]).then_inc(T.sem[s], 1)
        record(e, (s, count[s]), reads, writes)

    def sums(bank, calls):
        for n, (out, lhsT, rhs, reads) in enumerate(calls):
            depend("p", reads, [] if n else [(bank, 0, 512)])
            last = g.tensor.matmul(out, lhsT, rhs, n == 0, n == len(calls) - 1)
        count["qp"] = count.get("qp", 0) + 1
        last.then_inc(T.sem.qp, 1)
        record("p", ("qp", count["qp"]), [r for c in calls for r in c[3]], [(bank, 0, 512)])

    def dma(e, sem, out, in_, reads, writes):
        depend(e, reads, writes)
        count[sem] = count.get(sem, 0) + 16
        queue[e].dma_start(out, in_).then_inc(T.sem[sem], 16)
        record(e, (sem, count[sem]), reads, writes)

    later = [c for c in T.cores if T.rank_of(c) > rank]
    sent = [0]
    top = len(T.cores) - 1

    def lanes(src, dst):
        if topo.chip(src) != topo.chip(dst):
            return topo.engines(src, dst)
        off = [x for c in T.cores if topo.chip(c) != topo.chip(src) and T.rank_of(c) > T.rank_of(src)
               for x in topo.engines(src, c)]
        return [x for x in topo.engines(src, dst) if x not in off]

    def send(cores, name, lo, hi, sem, dst_name, dlo, dhi):
        if not cores:
            return
        depend("g", [(name, lo, hi)], [])
        sets = []
        for c in cores:
            e = lanes(core, c)
            same = [x for x in sets if x[0] == e]
            if same:
                same[0][1].append(c)
            else:
                sets.append([e, [c]])
        trs = []
        for e, cs in sets:
            ids = []
            for c in cs:
                rid, pid, _ = topo.addr(c)
                ids.append(DstId(rid=rid, pnc=pid))
            trs.append(RemoteDMATransfer(dst_ids=ids, dma_engine_mask=sum(1 << x for x in e), remote_sem=T.sem[sem],
                                         srcs=[T[name][:, lo:hi]], dsts=[T[dst_name][:, dlo:dhi] for _ in cs]))
            sent[0] += len(e)
        g.remote_dma_fused(trs, local_sem=T.sem.sent)

    A, F = AluOpType, ActivationFunctionType

    if rank:
        record(None, ("lea", sum(len(lanes(T.cores[s], core)) for s in range(rank))), [],
               [("D", NL * s, NL * s + NT) for s in range(rank)])
        for s in range(rank):
            if rank == top and s == top - 2:
                continue
            by = s - 1 if s == top - 1 else s
            record(None, ("m%d" % s, len(lanes(T.cores[by], core))), [], [("M", 32 * s, 32 * s + 32)])
    if rank == top - 2:
        record(None, ("m%d" % top, len(lanes(T.cores[top - 1], core))), [], [("M", 32 * top, 32 * top + 32)])

    dma("s", "ldln", T.lnI[0:8, :], T.ln[:], [], [("lnI", 0, 128)])
    dma("a", "ldle", T.D[:, NL * rank:NL * rank + NT], T.le[:], [], [("D", NL * rank, NL * rank + NT)])
    dma("s", "ldd0", T.dsI[0:8, :], T.ds[:], [], [("dsI", 0, 64)])
    dma("s", "ldd1", T.dsI[8:16, :], T.ds[:], [], [("dsI", 64, 128)])

    def iota(name, rows, n, pattern, cm):
        out = T[name][0:rows, 0:n]
        if name == "pI":
            op("g", lambda q: q.iota(out, pattern, 0, cm), [], [(name, 0, n)])
        else:
            op("g", lambda q: q.iota(out, pattern, 0, cm, allow_small_or_imprecise_dtypes=True), [], [(name, 0, n)])

    iota("pI", 128, 2, [[0, 2]], 1)
    iota("x", 128, 144, [[1, 144]], 0)
    iota("cS", 8, 128, [[1, 8], [0, 16]], -1)
    iota("r16", 128, 128, [[0, 8], [1, 16]], 0)

    send(later, "D", NL * rank, NL * rank + NT, "lea", "D", NL * rank, NL * rank + NT)

    def vs(out, in0, s1, s2, op0, op1, reads, writes):
        if op1 is None:
            op("v", lambda q: q.tensor_scalar(out, in0, s1, None, op0), reads, writes)
        else:
            op("v", lambda q: q.tensor_scalar(out, in0, s1, s2, op0, op1), reads, writes)

    def act(out, in_, func, reads, writes, bias=0.0, scale=1.0):
        op("a", lambda q: q.activation(out, in_, func, bias=bias, scale=scale), reads, writes)

    def col(name, rows=128):
        return T[name][0:rows, 0:1]

    def one(name):
        return (name, 0, 1)

    def vcol(name, src, s1, s2, op0, op1):
        vs(col(name), col(src), s1, s2, op0, op1, [one(src)], [one(name)])

    def block(name, first, lo, hi):
        n = lo // HALF
        act(T[name][:, lo - first:hi - first], T.x[:, lo - n * HALF:hi - n * HALF], F.Identity,
            [("x", lo - n * HALF, hi - n * HALF), one("sL"), ("hs", n, n + 1)], [(name, lo - first, hi - first)],
            bias=T.hs[:, n:n + 1], scale=col("sL"))

    def from_x(name, rows, cols, s1, s2, op0, op1):
        n, named = len(range(144)[cols]), isinstance(s2, str)
        vs(T[name][0:rows, 0:n], T.x[0:rows, cols], col(s1, rows), col(s2, rows) if named else s2, op0, op1,
           [("x", 0, 144), one(s1)] + ([one(s2)] if named else []), [(name, 0, n)])

    def zero():
        for lo in range(NT, NL, HALF):
            act(T.D[:, lo:lo + HALF], T.x[:], F.Copy, [("x", 0, HALF)], [("D", lo, lo + HALF)], scale=0.0)

    wide = slice(0, 144)
    rd = [("WP", 0, 144), ("WM", 0, 144), ("X", 0, 130)]
    zcut = [NL] + list(range(3 * HALF, NC, HALF)) + [NC]
    step = {
        "rtI": lambda: vcol("rtI", "pI", 15, None, A.bitwise_and, None),
        "qgI": lambda: vcol("qgI", "pI", 4, None, A.arith_shift_right, None),
        "lowX": lambda: vs(T.lowX[0:16, 0:2], T.pI[0:16, 0:2], 8.0, float(HALF), A.is_lt, A.mult, [("pI", 0, 2)], [("lowX", 0, 2)]),
        "p16": lambda: vcol("p16", "pI", 16.0, -125.0, A.mult, A.add),
        "sH": lambda: vcol("sH", "rtI", 4.0, -float(HALF), A.is_equal, A.mult),
        "sL": lambda: vcol("sL", "rtI", 5.0, -1.0, A.is_equal, A.mult),
        "pos": lambda: vcol("pos", "qgI", 16.0, 16.0, A.mult, A.add),
        "far": lambda: vcol("far", "rtI", 2.0, 1000.0, A.is_ge, A.mult),
        "rt": lambda: vcol("rt", "rtI", 0.0, None, A.add, None),
        "bias": lambda: vcol("bias", "rtI", 2.0, float(HALF), A.is_equal, A.mult),
        "posW": lambda: vs(col("posW", 16), col("lowX", 16), 127.0 / HALF, col("p16", 16), A.mult, A.add,
                           [one("lowX"), one("p16")], [one("posW")]),
        "X0": lambda: op("v", lambda q: q.tensor_copy(T.X[0:16, 0:130:129], T.lowX[0:16, 0:2]), [("lowX", 0, 2)],
                         [("X", 0, 1), ("X", 129, 130)]),
        "topX": lambda: act(col("topX", 16), col("lowX", 16), F.Copy, [one("lowX")], [one("topX")], bias=float(HALF)),
        "hs": lambda: act(T.hs[:, 0:8], T.x[:, 0:8], F.Copy, [("x", 0, 8), one("sH")], [("hs", 0, 8)], scale=col("sH")),
        "top": lambda: act(col("top"), col("far"), F.Identity, [one("far"), one("pos")], [one("top")], bias=col("pos")),
        "B": lambda: from_x("B", 128, slice(16, 144, 16), "pos", None, A.is_equal, None),
        "WP": lambda: from_x("WP", 16, wide, "posW", 1.0, A.is_equal, A.mult),
        "WM": lambda: from_x("WM", 16, wide, "posW", -1.0, A.is_equal, A.mult),
        "HP": lambda: from_x("HP", 128, wide, "top", None, A.is_ge, None),
        "HN": lambda: from_x("HN", 128, wide, "top", -1.0, A.is_ge, A.mult),
        "QS": lambda: from_x("QS", 128, wide, "top", "pos", A.min, A.is_equal),
        "Q": lambda: from_x("Q", 128, wide, "pos", None, A.is_equal, None),
        "Sel": lambda: vs(T.Sel[0:8, :], T.cS[0:8, :], 0.0, None, A.is_equal, None, [("cS", 0, 128)], [("Sel", 0, 128)]),
        "mask": lambda: vs(T.mask[:], T.r16[:], col("rt"), None, A.is_ge, None, [("r16", 0, 128), one("rt")], [("mask", 0, 128)]),
        "lnF": lambda: vs(T.lnF[0:8, :], T.lnI[0:8, :], 1.0, None, A.add, None, [("lnI", 0, 128)], [("lnF", 0, 128)]),
        "psA": lambda: sums("psA", [(T.psA[:, 0:128], T.lnF[0:8, :], T.Sel[0:8, :], [("lnF", 0, 128), ("Sel", 0, 128)])]),
        "AA": lambda: op("v", lambda q: q.tensor_tensor(T.AA[:], T.psA[:, 0:128], T.mask[:], A.mult),
                         [("psA", 0, 512), ("mask", 0, 128)], [("AA", 0, 128)]),
        "cum": lambda: op("v", lambda q: q.tensor_tensor_scan(T.cum[0:8, 16:144], T.lnF[0:8, :], T.lnF[0:8, :], 0.0, A.add, A.max),
                          [("lnF", 0, 128)], [("cum", 16, 144)]),
        "psE": lambda: sums("psE", [(T.psE[:, 0:8], T.AA[:], T.B[:], [("AA", 0, 128), ("B", 0, 8)]),
                                    (T.psE[:, 1:8], T.Sel[0:8, :], T.cum[0:8, 31:128:16], [("cum", 16, 144), ("Sel", 0, 128)])]),
        "offs": lambda: vs(T.offs[:], T.psE[:, 0:8], -1.0, None, A.add, None, [("psE", 0, 512)], [("offs", 0, 8)]),
        "X": lambda: vs(T.X[0:16, 1:129], T.dsI[0:16, :], col("lowX", 16), col("topX", 16), A.max, A.min,
                        [("dsI", 0, 128), one("lowX"), one("topX")], [("X", 1, 129)]),
        "psD": lambda: sums("psD", [(T.psD[:, 0:129], T.WP[0:16, 2:130], T.X[0:16, 1:130], rd),
                                    (T.psD[:, 0:129], T.WM[0:16, 2:130], T.X[0:16, 0:129], rd),
                                    (T.psD[:, 0:129], T.WM[0:16, 0:128], T.X[0:16, 1:130], rd)]),
        "tmp": lambda: act(T.tmp[:, 0:129], T.psD[:, 0:129], F.Identity, [("psD", 0, 512), one("bias")], [("tmp", 0, 129)],
                           bias=col("bias")),
        "scatter": lambda: op("v", lambda q: q.tensor_tensor(T.Z[:, 0:P].indirect(T.offs[:, 0:8]), T.tmp[:, 1:129], T.T0[:, 0:NT], A.add),
                              [("tmp", 1, 129), ("T0", 0, NT), ("offs", 0, 8)], [("Z", 0, P)]),
        "scan": lambda: op("v", lambda q: q.tensor_tensor_scan(T.T0[:, NL:NC], T.Z[:], T.Z[:], T.tmp[:, 0:1], A.add, A.max),
                           [("Z", 0, P), ("tmp", 0, 1)], [("T0", NL, NC)]),
        "zero": zero,
        "xb": lambda: act(T.x[:, 144:HALF], T.x[:, 0:HALF - 144], F.Copy, [("x", 0, 144)], [("x", 144, HALF)], bias=144.0),
    }
    for n in range(len(zcut) - 1):
        step["Z%d" % n] = lambda n=n: block("Z", NL, zcut[n], zcut[n + 1])
    for n, (name, lo, hi) in enumerate(FIXED):
        step["F%d" % n] = lambda a=(name, 0, lo, hi): block(*a)
    for name in ORDER.split():
        step[name]()

    wrapped, nbank = {}, [0]

    def bank():
        nbank[0] += 1
        return "psW%d" % (nbank[0] % 4)

    def wrap_first():
        b = wrapped[0] = bank()
        rz, rt = [("QS", 0, 144), ("Z", 0, P)], [("HP", 0, 144), ("HN", 0, 144), ("T0", NL, NC)]
        sums(b, [(T[b][:, 0:64], T.QS[:, 16 - k:144 - k], T.Z[:, k:P:16], rz) for k in range(16)]
             + [(T[b][:, 0:1], T.HP[:, 16:144], T.tmp[:, 0:1], [("HP", 0, 144), ("tmp", 0, 1)]),
                (T[b][:, 1:64], T.HP[:, 16:144], T.T0[:, NL + 15:NC - 16:16], rt),
                (T[b][:, 0:64], T.HN[:, 0:128], T.T0[:, NL + 15:NC:16], rt)])

    def wrap(n, tab=None, lo=NL, hi=NC):
        tab, b = tab or "T%d" % (n % 2), bank()
        wrapped[n] = b
        r = [("Q", 0, 144), (tab, lo, hi)]
        sums(b, [(T[b][:, 0:(hi - lo) // 16], T.Q[:, 16 - k:144 - k], T[tab][:, lo + k:hi:16], r) for k in range(16)])

    def turn(key, tab, first):
        b = wrapped[key] = bank()
        sums(b, [(T[b][:, 0:32], T.Q[:, 16 - k:144 - k], T[tab][:, first + 32 * k:first + 32 * k + 32],
                  [("Q", 0, 144), (tab, first + 32 * k, first + 32 * k + 32)]) for k in range(16)])

    def to_list(key, name, n=64):
        if key in wrapped:
            b = wrapped.pop(key)
            vs(T[name][:, 0:n], T[b][:, 0:n], -1.0, None, A.mult, None, [(b, 0, 512)], [(name, 0, n)])

    def gather(e, out, olo, win, wlo, whi, lst, c0, c1, o=None):
        i = T[win][:, wlo:whi].indirect(T[lst][:, c0:c1])
        if o is None:
            o = T[out][:, olo:olo + 16 * (c1 - c0)]
        r, w = [(win, wlo, whi), (lst, c0, c1)], [(out, olo, olo + 16 * (c1 - c0))]
        if e == "v":
            op("v", lambda q: q.tensor_copy(o, i), r, w)
        else:
            op("a", lambda q: q.activation(o, i, F.Copy), r, w)

    def both(out, olo, win, wlo, whi, lst, c0, c1):
        mid = (c0 + c1) // 2
        gather("v", out, olo, win, wlo, whi, lst, c0, mid)
        gather("a", out, olo + 16 * (mid - c0), win, wlo, whi, lst, mid, c1)

    def compose(n, lo, hi):
        m = PLAN[n - 1]
        to_list(m, "L%d" % (m % 3))
        both("T%d" % (n % 2), NL + lo, "T%d" % ((n - 1) % 2), 0, NC, "L%d" % (m % 3), lo // 16, hi // 16)

    last = len(PLAN)
    wrap_first()
    for n in range(1, last - 1):
        compose(n, 0, P)
        if n in PLAN:
            wrap(n)
    tab = "T%d" % ((last - 1) % 2)
    if later:
        for lo in (W, W + W // 2):
            compose(last - 1, lo, lo + W // 2)
        turn("t", tab, NL + W)
        compose(last - 1, 0, W)
        to_list("t", "LT", 32)
        for c in (0, 16):
            both("U", 16 * c, tab, 0, NC, "LT", c, c + 16)
        turn("m", "U", 0)
        to_list("m", "LM", 32)
        order = sorted(later, key=lambda c: -T.rank_of(c))
        slot = rank
        if rank == top - 2:
            order = order[1:]
        if rank == top - 1:
            order, slot = [T.cores[top - 2]], top
        for a, b in GROUPS:
            send(order[a:b], "LM", 0, 32, "m%d" % slot, "M", 32 * slot, 32 * slot + 32)
    else:
        compose(last - 1, 0, P)
    wrap(last - 1)
    if rank != top - 2:
        compose(last, 0, P)
        wrap(last)
    else:
        block("T0", 2 * NL - NC, NL, NL + NT)
        to_list(last - 1, "L1")
        gather("v", "T0", NL - NT, tab, 0, NC, "L1", 0, 32)
        gather("a", "T0", NL + W, tab, 0, NC, "L1", 32, 64)
        both("U", 0, "T0", NC - NL, NC, "M", 32 * top, 32 * top + 32)
        wrap("p", "U", 0, W)
        wrap(last, "T0", NL - NT, NC)

    for s in range(rank):
        at, lo, hi = NL * (s + 1) + NT, NL * s, NL * s + NL
        if rank == top and s == top - 2:
            continue
        if s == top - 1:
            lo, hi = lo - NL, lo + NT
        for h, e in enumerate("va"):
            gather(e, "D", at + h * W // 2, "D", lo, hi, "M", 32 * s + 16 * h, 32 * s + 16 * h + 16,
                   T.D[:, at + h:at + W:2])
        if rank != top - 2:
            to_list(last, "LF")
        elif s == 0:
            to_list("p", "LT", 32)
            send([T.cores[top]], "LT", 0, 32, "m%d" % (top - 1), "M", 32 * (top - 1), 32 * top)
        elif s == 1:
            b = wrapped.pop(last)
            for c, d in ((0, 0), (32, 40)):
                vs(T.LF[:, c:c + 32], T[b][:, d:d + 32], -1.0, None, A.mult, None, [(b, 0, 512)], [("LF", c, c + 32)])
    to_list(last, "LF")
    for h, (lo, hi) in enumerate(zip(CUTS, CUTS[1:])):
        both("Y", lo, "D", NL * rank, NL * rank + NL, "LF", lo // 16, hi // 16)
        dma("s", "st%d" % h, T.y[:, lo:hi], T.Y[:, lo:hi], [("Y", lo, hi)], [])
    for s in ("qv", "qa", "qp", "qg", "ldln", "ldd0", "ldd1", "ldle"):
        await_tokens("s", [(s, count[s])])
    if sent[0]:
        g.wait_ge(T.sem.sent, sent[0])
    await_tokens("s", [("st%d" % h, 16) for h in range(len(CUTS) - 1)])
